import numpy as np
import ml_dtypes


def mxq(x, axis, fmt="e4m3"):
    dtype, down = {"e4m3": (ml_dtypes.float8_e4m3fn, 7), "e5m2": (ml_dtypes.float8_e5m2, 14)}[fmt]
    v = np.moveaxis(np.asarray(x, np.float32).astype(ml_dtypes.bfloat16).astype(np.float64), axis, -1)
    blocks = v.reshape(v.shape[:-1] + (-1, 32))
    amax = np.abs(blocks).max(-1, keepdims=True)
    byte = np.maximum(np.where(amax > 0, np.frexp(amax)[1] - 1 + 127, 0) - down, 1)
    scale = np.exp2(byte - 127.0)
    codes = (blocks / scale).astype(np.float32).astype(dtype).astype(np.float64)
    return np.moveaxis((codes * scale).reshape(v.shape), -1, axis)


WIDE = False


def mx_kscale(k):
    if not WIDE:
        return np.ones(k)
    levels = np.array([10, -10, 5, -5, 0])
    if k % 512:
        return np.exp2(np.random.permutation(np.resize(levels, k // 32))).repeat(32)
    a = np.empty((k // 512, 16))
    for p in range(k // 512):
        a[p, :8] = np.random.permutation(np.resize(levels, 8))
        for g in range(8):
            far = levels[np.abs(levels - a[p, g]) >= 10]
            a[p, g + 8] = far[np.random.randint(len(far))]
    return np.exp2(a.ravel()).repeat(32)


def f64(x):
    return np.asarray(x).astype(np.float64)


def striped(idx):
    return np.tile(idx.reshape(-1, 16).T, (8, 1)).astype(np.uint16)


def unstriped(offs):
    return offs[:16].T.reshape(-1).astype(np.int64)


E2M1 = np.array([0.0, 0.5, 1.0, 1.5, 2.0, 3.0, 4.0, 6.0, -0.0, -0.5, -1.0, -1.5, -2.0, -3.0, -4.0, -6.0])


def pack_weight(w, fmt):
    k, n = w.shape
    w = f64(np.asarray(w, np.float32).astype(ml_dtypes.bfloat16)).reshape(k // 32, 32, n)
    amax = np.abs(w).max(1)
    if fmt == "e4m3":
        byte = np.frexp(amax)[1] - 1 + 127 - 7
    else:
        mant, ex = np.frexp(amax / 6.0)
        byte = np.where(mant > 0.5, ex, ex - 1) + 127
    byte = np.clip(np.where(amax > 0, byte, 1), 1, 254)
    scaled = (w * np.exp2(127.0 - byte)[:, None, :]).reshape(k, n).astype(np.float32)
    by_word = np.ascontiguousarray(scaled.reshape(k // 512, 128, 4, n).transpose(0, 1, 3, 2))
    if fmt == "e4m3":
        words = by_word.astype(ml_dtypes.float8_e4m3fn).view(np.uint8)
    else:
        c = by_word.astype(ml_dtypes.float4_e2m1fn).view(np.uint8) & 0xF
        words = (c[..., 0::2] | (c[..., 1::2] << 4)).reshape(k // 512, 128, 2 * n)
    return np.ascontiguousarray(words), np.ascontiguousarray(byte.astype(np.uint8).reshape(k // 512, 16, n))


def unpack_weight(words, scales, fmt):
    g, _, n = scales.shape
    words = np.ascontiguousarray(words).reshape(g, 128, n, -1)
    if fmt == "e4m3":
        vals = words.view(ml_dtypes.float8_e4m3fn).astype(np.float64)
    else:
        nib = np.empty((g, 128, n, 4), np.uint8)
        nib[..., 0::2] = words & 0xF
        nib[..., 1::2] = words >> 4
        vals = E2M1[nib]
    vals = vals * np.repeat(np.exp2(scales.astype(np.float64) - 127.0), 8, axis=1)[..., None]
    return vals.transpose(0, 1, 3, 2).reshape(g * 512, n)


def gelu(v):
    return 0.5 * v * (1.0 + np.tanh(np.sqrt(2.0 / np.pi) * (v + 0.044715 * v**3)))


def striped8(idx):
    return np.concatenate([v.reshape(-1, 16).T for v in idx]).astype(np.uint16)


def unstriped8(offs):
    return np.stack([offs[16 * g:16 * g + 16].T.reshape(-1) for g in range(8)]).astype(np.int64)


def runs(v, idx8):
    k = np.arange(v.shape[0])
    return v[k[:, None], idx8[k % 512 // 64]]


K, T, S, P, H, N = 1024, 2048, 1024, 512, 1024, 384

def setup_inputs():
    n = np.random.standard_normal
    s = mx_kscale(K)[:, None]
    u = mx_kscale(H)[:, None]
    d = {}
    d["tab_words"], d["tab_scales"] = pack_weight(n((K, T)) * s, "e4m3")
    d["offs"] = striped8(np.stack([np.random.permutation(T)[:S] for _ in range(8)]))
    perm = np.random.permutation(S)
    d["pos1"] = striped(perm[:P])
    d["pos2"] = striped(perm[S - P:])
    d["w1"] = (n((K, H)) / K ** 0.5 / s).astype(np.float32)
    d["gain"] = (np.exp(0.3 * n(H)) * u[:, 0]).astype(np.float32)
    d["cap"] = (np.random.uniform(0.2, 2.0, (H, P)) * u).astype(np.float32)
    d["w2_words"], d["w2_scales"] = pack_weight(0.24 * n((H, N)) / H ** 0.5 / u, "e2m1")
    d["w3"] = (0.42 * n((H, N)) / H ** 0.5 / u).astype(np.float32)
    d["bias"] = (0.15 * n(N)).astype(np.float32)
    return d

def reference(tab_words, tab_scales, offs, pos1, pos2, w1, gain, cap, w2_words, w2_scales, w3, bias):
    v = runs(unpack_weight(tab_words, tab_scales, "e4m3"), unstriped8(offs))
    h = f64(gain)[:, None] * (mxq(f64(w1), 0, "e4m3").T @ v)
    dif = np.abs(h[:, unstriped(pos1)] - h[:, unstriped(pos2)])
    low = np.minimum(dif, f64(cap))
    difq = mxq(dif, 0, "e4m3")
    lowq = mxq(low, 0, "e4m3")
    w2 = unpack_weight(w2_words, w2_scales, "e2m1")
    y = w2.T @ difq + mxq(f64(w3), 0, "e4m3").T @ lowq
    return np.sin(y + f64(bias)[:, None])

@@ -1,0 +1,302 @@
+from contextlib import ExitStack
+
+import concourse.mybir as mybir
+
+K, T, S, M, H, N = 1024, 2048, 1024, 512, 1024, 384
+FLOPS = 2 * K * H * S + 2 * 2 * H * N * M
+
+F32 = mybir.dt.float32
+BF16 = mybir.dt.bfloat16
+I32 = mybir.dt.int32
+U32 = mybir.dt.uint32
+U16 = mybir.dt.uint16
+U8 = mybir.dt.uint8
+FP8X4 = mybir.dt.float8_e4m3fn_x4
+FP4X4 = mybir.dt.float4_e2m1fn_x4
+ALU = mybir.AluOpType
+ACT = mybir.ActivationFunctionType
+
+P = 128
+PACK = 4
+PASS = P * PACK
+BANK = 512
+HALF = M // 2
+VECTOR_SHARE = 64
+
+
+def tile_list_signature_skew_features_kernel(
+    tc, tab_words, tab_scales, offs, pos1, pos2, w1, gain, cap, w2_words, w2_scales, w3, bias, out
+):
+    nc = tc.nc
+    with ExitStack() as ctx:
+        keep = ctx.enter_context(tc.tile_pool(name="keep", bufs=1))
+        ring = ctx.enter_context(tc.tile_pool(name="ring", bufs=3))
+        psum = ctx.enter_context(tc.psum_pool(name="psum", bufs=1))
+
+        def held(shape, dtype, name):
+            return keep.tile(shape, dtype, name=name, align_bytes=64)
+
+        offs_t = keep.tile([P, S // 16], U16, name="offs_t")
+        pos1_t = keep.tile([P, M // 16], U16, name="pos1_t")
+        pos2_t = keep.tile([P, M // 16], U16, name="pos2_t")
+        nc.sync.dma_start(offs_t[:], offs)
+        nc.sync.dma_start(pos1_t[:], pos1)
+        nc.sync.dma_start(pos2_t[:], pos2)
+
+        tab_rows = held([P, T], U8, "tab_rows")
+        nc.vector.memset(tab_rows[:].bitcast(I32), 0)
+        by_row = tab_scales.rearrange("a (g r) t -> r g a t", r=2)
+        for r in range(2):
+            nc.scalar.dma_start(tab_rows[:].bitcast(I32)[r:P:8, :], by_row[r].bitcast(I32))
+
+        zero_in = held([P, 1], F32, "late")
+        zero = held([P, 1], F32, "zero")
+        nc.vector.memset(zero_in[:], 0.0)
+        nc.scalar.activation(zero[:], zero_in[:], ACT.Sin)
+
+        tab, w1_raw, cap_t = {}, {}, {}
+
+        def load_tab(a):
+            tab[a] = ring.tile([P, T], I32, name="loaded", align_bytes=64)
+            nc.sync.dma_start(tab[a][:], tab_words[a].rearrange("p t i -> p (t i)").bitcast(I32))
+
+        def load_rows(src, a, lo, hi, pool=ring, name="loaded"):
+            dst = pool.tile([P, PACK, hi - lo], F32, name=name, align_bytes=64)
+            nc.sync.dma_start(dst[:], src[a * PASS : (a + 1) * PASS, lo:hi].rearrange("(p j) c -> p j c", j=PACK))
+            return dst
+
+        load_tab(0)
+        w1_raw[0, 0] = load_rows(w1, 0, 0, PASS)
+        load_tab(1)
+        w1_raw[0, 1] = load_rows(w1, 1, 0, PASS, keep, "late")
+
+        gain_t = held([P, 2, PACK], F32, "gain_t")
+        nc.gpsimd.dma_start(gain_t[:], gain.rearrange("(b p t) -> p b t", p=P, t=PACK))
+        w2_planes = held([P, 2, N], U8, "w2_planes")
+        w2_planes_i = w2_planes[:].rearrange("p a c -> p (a c)").bitcast(I32)
+        nc.gpsimd.memset(w2_planes_i, 0)
+        w2_codes = held([P, 2, 2 * N], U8, "w2_codes")
+        bias_t = held([P, N // P], F32, "bias_t")
+
+        picked_rows = held([P, S], U8, "picked_rows")
+        nc.vector.tensor_copy(picked_rows[:], tab_rows[:].indirect(offs_t[:]))
+        v_planes = held([P, S], U8, "v_planes")
+        nc.vector.tensor_copy(v_planes[:].bitcast(I32), picked_rows[:].bitcast(I32))
+        for a in range(2):
+            for r in range(2):
+                nc.sync.dma_start(
+                    v_planes[:].bitcast(I32)[8 * a + 2 + r : P : 32, :],
+                    picked_rows[:].bitcast(I32)[16 + 8 * a + r : P : 32, :],
+                )
+        nc.gpsimd.dma_start(w2_codes[:].bitcast(I32), w2_words.rearrange("a p c -> p a c").bitcast(I32))
+        w2_by_row = w2_scales.rearrange("a (d r) c -> r d a c", r=4)
+        for r in range(4):
+            nc.gpsimd.dma_start(w2_planes[:].bitcast(I32)[r:P:32, :, :], w2_by_row[r].bitcast(I32))
+        with nc.allow_non_contiguous_dma(reason="one bias value for each partition"):
+            nc.gpsimd.dma_start(bias_t[:], bias.rearrange("(c p) -> p c", p=P))
+
+        v_words = [held([P, S], U32, f"v_words{a}") for a in range(2)]
+
+        def pick_words(a):
+            nc.vector.tensor_copy(v_words[a][:], tab[a][:].bitcast(U32).indirect(offs_t[:]))
+
+        w1_keys = [(b, a) for b in range(2) for a in range(2)]
+        w1_bf = {key: held([P, PACK, P, PACK], BF16, f"w1_bf{key[0]}{key[1]}") for key in w1_keys}
+        w1_codes = {key: held([P, PASS], U32, f"w1_codes{key[0]}{key[1]}") for key in w1_keys}
+        w1_planes = {key: held([P, PASS], U8, f"w1_planes{key[0]}{key[1]}") for key in w1_keys}
+
+        def round_w1(copy, key, ms):
+            copy(
+                w1_bf[key][:, :, ms, :].rearrange("p t m j -> p m j t"),
+                w1_raw[key][:].rearrange("p j (m t) -> p m j t", t=PACK)[:, ms, :, :],
+            )
+
+        def quantize(codes, planes, rounded, lo, hi):
+            nc.vector.quantize_mx(
+                out=codes[:, lo:hi].bitcast(FP8X4), scales=planes[:, lo:hi], in_=rounded[:, PACK * lo : PACK * hi]
+            )
+
+        def quantize_w1(key, lo, hi):
+            quantize(w1_codes[key], w1_planes[key], w1_bf[key][:].rearrange("p t m j -> p (t m j)"), lo, hi)
+
+        h = {}
+
+        def first_stage(b, t, second_half_on_vector=False):
+            h[b, t] = held([P, S], F32, f"h{b}{t}")
+            cols = slice(t * P, (t + 1) * P)
+            for u in range(S // BANK):
+                acc = psum.tile([P, BANK], F32, name=f"bank{(2 * t + u) % 8}")
+                picked = slice(u * BANK, (u + 1) * BANK)
+                passes = (0, 1) if t == 0 else (1, 0)
+                for a in passes:
+                    nc.tensor.matmul_mx(
+                        acc[:],
+                        lhsT=w1_codes[b, a][:, cols].bitcast(FP8X4),
+                        lhsT_scale=w1_planes[b, a][:, cols],
+                        rhs=v_words[a][:, picked].bitcast(FP8X4),
+                        rhs_scale=v_planes[8 * a : P, picked],
+                        start=(a == passes[0]),
+                        stop=(a == passes[1]),
+                    )
+                if u == 1 and second_half_on_vector:
+                    nc.vector.tensor_scalar_mul(h[b, t][:, picked], acc[:], gain_t[:, b, t : t + 1])
+                else:
+                    nc.scalar.activation(h[b, t][:, picked], acc[:], ACT.Copy, scale=gain_t[:, b, t : t + 1])
+
+        units = [(b, lo, lo + HALF) for b in range(2) for lo in (0, HALF)]
+        signed = {u: held([P, PACK, u[2] - u[1]], F32, f"signed{i}") for i, u in enumerate(units)}
+        dif = {u: held([P, PACK, u[2] - u[1]], F32, f"dif{i}") for i, u in enumerate(units)}
+        dif_bf = {u: held([P, u[2] - u[1], PACK], BF16, f"dif_bf{i}") for i, u in enumerate(units)}
+        low_bf = {u: held([P, u[2] - u[1], PACK], BF16, f"low_bf{i}") for i, u in enumerate(units)}
+        dif_codes = [held([P, M], U32, f"dif_codes{b}") for b in range(2)]
+        low_codes = [held([P, M], U32, f"low_codes{b}") for b in range(2)]
+        dif_planes = [held([P, M], U8, f"dif_planes{b}") for b in range(2)]
+        low_planes = [held([P, M], U8, f"low_planes{b}") for b in range(2)]
+
+        def subtract_pairs(b, t):
+            second = {}
+            for u in units[2 * b : 2 * b + 2]:
+                second[u] = ring.tile([P, HALF], F32, name="second", bufs=4)
+                nc.vector.tensor_copy(second[u][:], h[b, t][:].indirect(pos2_t[:, u[1] // 16 : u[2] // 16]))
+            for u in units[2 * b : 2 * b + 2]:
+                nc.vector.tensor_tensor(
+                    signed[u][:, t, :],
+                    h[b, t][:].indirect(pos1_t[:, u[1] // 16 : u[2] // 16]),
+                    second[u][:],
+                    ALU.subtract,
+                )
+
+        def take_abs(u, t):
+            nc.scalar.activation(dif[u][:, t, :], signed[u][:, t, :], ACT.Abs, bias=zero[:])
+
+        def pairs_in(rows):
+            return rows.rearrange("p t (c i) -> p c t i", i=2)
+
+        def pairs_out(words):
+            return words.rearrange("p (c i) t -> p c t i", i=2)
+
+        def round_dif(u):
+            nc.scalar.activation(pairs_out(dif_bf[u][:]), pairs_in(signed[u][:]), ACT.Abs, bias=zero[:])
+
+        def round_low(u):
+            b, lo, hi = u
+            nc.vector.tensor_tensor(pairs_out(low_bf[u][:]), pairs_in(dif[u][:]), pairs_in(cap_t[b][:, :, lo:hi]), ALU.min)
+
+        def quantize_unit(codes, planes, rounded, u):
+            b, lo, hi = u
+            quantize(codes[b][:, lo:hi], planes[b][:, lo:hi], rounded[u][:].rearrange("p m t -> p (m t)"), 0, hi - lo)
+
+        w3_bf = held([P, 2, N, PACK], BF16, "w3_bf")
+        w3_codes = held([P, 2 * N], U32, "w3_codes")
+        w3_planes = held([P, 2 * N], U8, "w3_planes")
+
+        y = {}
+
+        def second_stage(b, half, c):
+            lo = half * HALF
+            if b == 0:
+                y[half, c] = psum.tile([P, HALF], F32, name=f"bank{3 * half + c}")
+            acc = y[half, c]
+
+            def low_pass():
+                w3_cols = slice(b * N + c * P, b * N + (c + 1) * P)
+                nc.tensor.matmul_mx(
+                    acc[:],
+                    lhsT=w3_codes[:, w3_cols].bitcast(FP8X4),
+                    lhsT_scale=w3_planes[:, w3_cols],
+                    rhs=low_codes[b][:, lo : lo + HALF].bitcast(FP8X4),
+                    rhs_scale=low_planes[b][:, lo : lo + HALF],
+                    start=(b == 0),
+                    stop=(b == 1),
+                )
+
+            if b == 0:
+                low_pass()
+            for m0 in range(0, HALF, P):
+                nc.tensor.matmul_mx(
+                    acc[:, m0 : m0 + P],
+                    lhsT=w2_codes[:, b, 2 * c * P : 2 * (c + 1) * P].bitcast(FP4X4),
+                    lhsT_scale=w2_planes[:, b, c * P : (c + 1) * P],
+                    rhs=dif_codes[b][:, lo + m0 : lo + m0 + P].bitcast(FP8X4),
+                    rhs_scale=dif_planes[b][:, lo + m0 : lo + m0 + P],
+                    start=False,
+                    stop=False,
+                )
+            if b == 1:
+                low_pass()
+
+        out_rows = out.rearrange("(c p) m -> p c m", p=P)
+
+        def finish(half):
+            result = held([P, N // P, HALF], F32, f"result{half}")
+            cols = slice(half * HALF, (half + 1) * HALF)
+            for c in range(N // P):
+                second_stage(1, half, c)
+                nc.scalar.activation(result[:, c, :], y[half, c][:], ACT.Sin, bias=bias_t[:, c : c + 1])
+                nc.sync.dma_start(out_rows[:, c, cols], result[:, c, :])
+
+        whole = slice(0, P)
+        pick_words(0)
+        w1_raw[1, 0] = load_rows(w1, 0, PASS, 2 * PASS)
+        round_w1(nc.scalar.copy, (0, 0), whole)
+        w1_raw[1, 1] = load_rows(w1, 1, PASS, 2 * PASS)
+        pick_words(1)
+        cap_t[0] = load_rows(cap, 0, 0, M)
+        quantize_w1((0, 0), 0, PASS)
+        round_w1(nc.vector.tensor_copy, (0, 1), slice(0, VECTOR_SHARE))
+        round_w1(nc.scalar.copy, (0, 1), slice(VECTOR_SHARE, P))
+        w3_raw = held([P, 2, PACK, N], F32, "late")
+        nc.sync.dma_start(w3_raw[:], w3.rearrange("(b p j) n -> p b j n", p=P, j=PACK))
+        quantize_w1((0, 1), 0, P)
+        quantize_w1((0, 1), P, 2 * P)
+        quantize_w1((0, 1), 2 * P, PASS)
+        def round_w1_in_pieces(key):
+            for m0 in range(0, P, 32):
+                round_w1(nc.scalar.copy, key, slice(m0, m0 + 32))
+
+        first_stage(0, 0, second_half_on_vector=True)
+        first_stage(0, 1)
+        round_w1_in_pieces((1, 0))
+        cap_t[1] = load_rows(cap, 1, 0, M)
+        quantize_w1((1, 0), 0, PASS)
+        first_stage(0, 2)
+        round_w1_in_pieces((1, 1))
+        quantize_w1((1, 1), 0, PASS)
+        first_stage(0, 3)
+        for t in range(PACK):
+            subtract_pairs(0, t)
+        first_stage(1, 0)
+        for t in range(PACK):
+            for u in units[:2]:
+                take_abs(u, t)
+        first_stage(1, 1)
+        for u in units[:2]:
+            round_low(u)
+        for u in units[:2]:
+            round_dif(u)
+        first_stage(1, 2)
+        nc.scalar.copy(pairs_out(w3_bf[:, 0, :, :]), pairs_in(w3_raw[:, 0, :, :]))
+        nc.scalar.copy(pairs_out(w3_bf[:, 1, :, :]), pairs_in(w3_raw[:, 1, :, :]))
+        first_stage(1, 3)
+        w3_flat = w3_bf[:].rearrange("p b n j -> p (b n j)")
+        quantize(w3_codes, w3_planes, w3_flat, 0, PASS)
+        quantize(w3_codes, w3_planes, w3_flat, PASS, 2 * N)
+        for u in units[:2]:
+            quantize_unit(low_codes, low_planes, low_bf, u)
+            quantize_unit(dif_codes, dif_planes, dif_bf, u)
+        for half in range(2):
+            for c in range(N // P):
+                second_stage(0, half, c)
+        for t in range(PACK):
+            subtract_pairs(1, t)
+        for u in units[2:]:
+            for t in range(PACK):
+                take_abs(u, t)
+            round_dif(u)
+        for half in range(2):
+            u = units[2 + half]
+            round_low(u)
+            quantize_unit(dif_codes, dif_planes, dif_bf, u)
+            quantize_unit(low_codes, low_planes, low_bf, u)
+        for half in range(2):
+            finish(half)

@@ -21,7 +21,7 @@ PACK = 4
 PASS = P * PACK
 BANK = 512
 HALF = M // 2
-VECTOR_SHARE = 64
+VECTOR_SHARE = 72
 
 
 def tile_list_signature_skew_features_kernel(
@@ -44,14 +44,14 @@ def tile_list_signature_skew_features_kernel(
         nc.sync.dma_start(pos2_t[:], pos2)
 
         tab_rows = held([P, T], U8, "tab_rows")
-        nc.vector.memset(tab_rows[:].bitcast(I32), 0)
+        nc.gpsimd.memset(tab_rows[:].bitcast(I32), 0)
         by_row = tab_scales.rearrange("a (g r) t -> r g a t", r=2)
         for r in range(2):
             nc.scalar.dma_start(tab_rows[:].bitcast(I32)[r:P:8, :], by_row[r].bitcast(I32))
 
         zero_in = held([P, 1], F32, "late")
         zero = held([P, 1], F32, "zero")
-        nc.vector.memset(zero_in[:], 0.0)
+        nc.gpsimd.memset(zero_in[:], 0.0)
         nc.scalar.activation(zero[:], zero_in[:], ACT.Sin)
 
         tab, w1_raw, cap_t = {}, {}, {}
@@ -72,11 +72,6 @@ def tile_list_signature_skew_features_kernel(
 
         gain_t = held([P, 2, PACK], F32, "gain_t")
         nc.gpsimd.dma_start(gain_t[:], gain.rearrange("(b p t) -> p b t", p=P, t=PACK))
-        w2_planes = held([P, 2, N], U8, "w2_planes")
-        w2_planes_i = w2_planes[:].rearrange("p a c -> p (a c)").bitcast(I32)
-        nc.gpsimd.memset(w2_planes_i, 0)
-        w2_codes = held([P, 2, 2 * N], U8, "w2_codes")
-        bias_t = held([P, N // P], F32, "bias_t")
 
         picked_rows = held([P, S], U8, "picked_rows")
         nc.vector.tensor_copy(picked_rows[:], tab_rows[:].indirect(offs_t[:]))
@@ -84,16 +79,10 @@ def tile_list_signature_skew_features_kernel(
         nc.vector.tensor_copy(v_planes[:].bitcast(I32), picked_rows[:].bitcast(I32))
         for a in range(2):
             for r in range(2):
-                nc.sync.dma_start(
+                nc.scalar.dma_start(
                     v_planes[:].bitcast(I32)[8 * a + 2 + r : P : 32, :],
                     picked_rows[:].bitcast(I32)[16 + 8 * a + r : P : 32, :],
                 )
-        nc.gpsimd.dma_start(w2_codes[:].bitcast(I32), w2_words.rearrange("a p c -> p a c").bitcast(I32))
-        w2_by_row = w2_scales.rearrange("a (d r) c -> r d a c", r=4)
-        for r in range(4):
-            nc.gpsimd.dma_start(w2_planes[:].bitcast(I32)[r:P:32, :, :], w2_by_row[r].bitcast(I32))
-        with nc.allow_non_contiguous_dma(reason="one bias value for each partition"):
-            nc.gpsimd.dma_start(bias_t[:], bias.rearrange("(c p) -> p c", p=P))
 
         v_words = [held([P, S], U32, f"v_words{a}") for a in range(2)]
 
@@ -250,15 +239,26 @@ def tile_list_signature_skew_features_kernel(
         quantize_w1((0, 1), 0, P)
         quantize_w1((0, 1), P, 2 * P)
         quantize_w1((0, 1), 2 * P, PASS)
-        def round_w1_in_pieces(key):
-            for m0 in range(0, P, 32):
+        def round_w1_in_pieces(key, first=0):
+            for m0 in range(first, P, 32):
                 round_w1(nc.scalar.copy, key, slice(m0, m0 + 32))
 
         first_stage(0, 0, second_half_on_vector=True)
+        round_w1(nc.vector.tensor_copy, (1, 0), slice(0, P // 2))
         first_stage(0, 1)
-        round_w1_in_pieces((1, 0))
+        round_w1_in_pieces((1, 0), P // 2)
         cap_t[1] = load_rows(cap, 1, 0, M)
         quantize_w1((1, 0), 0, PASS)
+        w2_codes = held([P, 2, 2 * N], U8, "w1_bf00")
+        nc.sync.dma_start(w2_codes[:].bitcast(I32), w2_words.rearrange("a p c -> p a c").bitcast(I32))
+        w2_planes = held([P, 2, N], U8, "w1_bf01")
+        nc.gpsimd.memset(w2_planes[:].rearrange("p a c -> p (a c)").bitcast(I32), 0)
+        w2_by_row = w2_scales.rearrange("a (d r) c -> r d a c", r=4)
+        for r in range(4):
+            nc.sync.dma_start(w2_planes[:].bitcast(I32)[r:P:32, :, :], w2_by_row[r].bitcast(I32))
+        bias_t = held([P, N // P], F32, "w1_bf10")
+        with nc.allow_non_contiguous_dma(reason="one bias value for each partition"):
+            nc.sync.dma_start(bias_t[:], bias.rearrange("(c p) -> p c", p=P))
         first_stage(0, 2)
         round_w1_in_pieces((1, 1))
         quantize_w1((1, 1), 0, PASS)
@@ -289,9 +289,11 @@ def tile_list_signature_skew_features_kernel(
                 second_stage(0, half, c)
         for t in range(PACK):
             subtract_pairs(1, t)
-        for u in units[2:]:
-            for t in range(PACK):
+        for t in range(PACK - 1):
+            for u in units[2:]:
                 take_abs(u, t)
+        for u in units[2:]:
+            take_abs(u, PACK - 1)
             round_dif(u)
         for half in range(2):
             u = units[2 + half]

@@ -21,7 +21,7 @@ PACK = 4
 PASS = P * PACK
 BANK = 512
 HALF = M // 2
-VECTOR_SHARE = 72
+VECTOR_SHARE = 64
 
 
 def tile_list_signature_skew_features_kernel(
@@ -30,7 +30,7 @@ def tile_list_signature_skew_features_kernel(
     nc = tc.nc
     with ExitStack() as ctx:
         keep = ctx.enter_context(tc.tile_pool(name="keep", bufs=1))
-        ring = ctx.enter_context(tc.tile_pool(name="ring", bufs=3))
+        ring = ctx.enter_context(tc.tile_pool(name="ring", bufs=2))
         psum = ctx.enter_context(tc.psum_pool(name="psum", bufs=1))
 
         def held(shape, dtype, name):
@@ -42,22 +42,24 @@ def tile_list_signature_skew_features_kernel(
         nc.sync.dma_start(offs_t[:], offs)
         nc.sync.dma_start(pos1_t[:], pos1)
         nc.sync.dma_start(pos2_t[:], pos2)
+        gain_t = held([P, 2, PACK], F32, "gain_t")
+        nc.sync.dma_start(gain_t[:], gain.rearrange("(b p t) -> p b t", p=P, t=PACK))
 
         tab_rows = held([P, T], U8, "tab_rows")
         nc.gpsimd.memset(tab_rows[:].bitcast(I32), 0)
         by_row = tab_scales.rearrange("a (g r) t -> r g a t", r=2)
         for r in range(2):
-            nc.scalar.dma_start(tab_rows[:].bitcast(I32)[r:P:8, :], by_row[r].bitcast(I32))
+            nc.sync.dma_start(tab_rows[:].bitcast(I32)[r:P:8, :], by_row[r].bitcast(I32))
 
-        zero_in = held([P, 1], F32, "late")
+        zero_in = held([P, 1], F32, "zero_in")
         zero = held([P, 1], F32, "zero")
         nc.gpsimd.memset(zero_in[:], 0.0)
         nc.scalar.activation(zero[:], zero_in[:], ACT.Sin)
 
         tab, w1_raw, cap_t = {}, {}, {}
 
-        def load_tab(a):
-            tab[a] = ring.tile([P, T], I32, name="loaded", align_bytes=64)
+        def load_tab(a, pool, name):
+            tab[a] = pool.tile([P, T], I32, name=name, align_bytes=64)
             nc.sync.dma_start(tab[a][:], tab_words[a].rearrange("p t i -> p (t i)").bitcast(I32))
 
         def load_rows(src, a, lo, hi, pool=ring, name="loaded"):
@@ -65,13 +67,16 @@ def tile_list_signature_skew_features_kernel(
             nc.sync.dma_start(dst[:], src[a * PASS : (a + 1) * PASS, lo:hi].rearrange("(p j) c -> p j c", j=PACK))
             return dst
 
-        load_tab(0)
+        load_tab(0, keep, "first")
         w1_raw[0, 0] = load_rows(w1, 0, 0, PASS)
-        load_tab(1)
+        load_tab(1, ring, "loaded")
         w1_raw[0, 1] = load_rows(w1, 1, 0, PASS, keep, "late")
 
-        gain_t = held([P, 2, PACK], F32, "gain_t")
-        nc.gpsimd.dma_start(gain_t[:], gain.rearrange("(b p t) -> p b t", p=P, t=PACK))
+
+        v_words = [held([P, S], U32, f"v_words{a}") for a in range(2)]
+
+        def pick_words(a):
+            nc.vector.tensor_copy(v_words[a][:], tab[a][:].bitcast(U32).indirect(offs_t[:]))
 
         picked_rows = held([P, S], U8, "picked_rows")
         nc.vector.tensor_copy(picked_rows[:], tab_rows[:].indirect(offs_t[:]))
@@ -79,22 +84,16 @@ def tile_list_signature_skew_features_kernel(
         nc.vector.tensor_copy(v_planes[:].bitcast(I32), picked_rows[:].bitcast(I32))
         for a in range(2):
             for r in range(2):
-                nc.scalar.dma_start(
+                nc.sync.dma_start(
                     v_planes[:].bitcast(I32)[8 * a + 2 + r : P : 32, :],
                     picked_rows[:].bitcast(I32)[16 + 8 * a + r : P : 32, :],
                 )
 
-        v_words = [held([P, S], U32, f"v_words{a}") for a in range(2)]
-
-        def pick_words(a):
-            nc.vector.tensor_copy(v_words[a][:], tab[a][:].bitcast(U32).indirect(offs_t[:]))
-
-        w1_keys = [(b, a) for b in range(2) for a in range(2)]
-        w1_bf = {key: held([P, PACK, P, PACK], BF16, f"w1_bf{key[0]}{key[1]}") for key in w1_keys}
-        w1_codes = {key: held([P, PASS], U32, f"w1_codes{key[0]}{key[1]}") for key in w1_keys}
-        w1_planes = {key: held([P, PASS], U8, f"w1_planes{key[0]}{key[1]}") for key in w1_keys}
+        w1_bf, w1_codes, w1_planes = {}, {}, {}
 
         def round_w1(copy, key, ms):
+            if key not in w1_bf:
+                w1_bf[key] = held([P, PACK, P, PACK], BF16, f"w1_{key[0]}{key[1]}")
             copy(
                 w1_bf[key][:, :, ms, :].rearrange("p t m j -> p m j t"),
                 w1_raw[key][:].rearrange("p j (m t) -> p m j t", t=PACK)[:, ms, :, :],
@@ -105,14 +104,20 @@ def tile_list_signature_skew_features_kernel(
                 out=codes[:, lo:hi].bitcast(FP8X4), scales=planes[:, lo:hi], in_=rounded[:, PACK * lo : PACK * hi]
             )
 
-        def quantize_w1(key, lo, hi):
-            quantize(w1_codes[key], w1_planes[key], w1_bf[key][:].rearrange("p t m j -> p (t m j)"), lo, hi)
+        def quantize_w1(key, t_lo, t_hi, name):
+            width = (t_hi - t_lo) * P
+            codes = held([P, width], U32, name)
+            planes = held([P, width], U8, name + "_planes")
+            quantize(codes, planes, w1_bf[key][:, t_lo:t_hi].rearrange("p t m j -> p (t m j)"), 0, width)
+            for t in range(t_lo, t_hi):
+                cols = slice((t - t_lo) * P, (t - t_lo + 1) * P)
+                w1_codes[key + (t,)] = codes[:, cols]
+                w1_planes[key + (t,)] = planes[:, cols]
 
         h = {}
 
         def first_stage(b, t, second_half_on_vector=False):
             h[b, t] = held([P, S], F32, f"h{b}{t}")
-            cols = slice(t * P, (t + 1) * P)
             for u in range(S // BANK):
                 acc = psum.tile([P, BANK], F32, name=f"bank{(2 * t + u) % 8}")
                 picked = slice(u * BANK, (u + 1) * BANK)
@@ -120,8 +125,8 @@ def tile_list_signature_skew_features_kernel(
                 for a in passes:
                     nc.tensor.matmul_mx(
                         acc[:],
-                        lhsT=w1_codes[b, a][:, cols].bitcast(FP8X4),
-                        lhsT_scale=w1_planes[b, a][:, cols],
+                        lhsT=w1_codes[b, a, t].bitcast(FP8X4),
+                        lhsT_scale=w1_planes[b, a, t],
                         rhs=v_words[a][:, picked].bitcast(FP8X4),
                         rhs_scale=v_planes[8 * a : P, picked],
                         start=(a == passes[0]),
@@ -226,42 +231,41 @@ def tile_list_signature_skew_features_kernel(
 
         whole = slice(0, P)
         pick_words(0)
-        w1_raw[1, 0] = load_rows(w1, 0, PASS, 2 * PASS)
         round_w1(nc.scalar.copy, (0, 0), whole)
-        w1_raw[1, 1] = load_rows(w1, 1, PASS, 2 * PASS)
+        w1_raw[1, 0] = load_rows(w1, 0, PASS, 2 * PASS)
         pick_words(1)
-        cap_t[0] = load_rows(cap, 0, 0, M)
-        quantize_w1((0, 0), 0, PASS)
+        w1_raw[1, 1] = load_rows(w1, 1, PASS, 2 * PASS)
+        quantize_w1((0, 0), 0, PACK, "w1_codes00")
         round_w1(nc.vector.tensor_copy, (0, 1), slice(0, VECTOR_SHARE))
         round_w1(nc.scalar.copy, (0, 1), slice(VECTOR_SHARE, P))
-        w3_raw = held([P, 2, PACK, N], F32, "late")
-        nc.sync.dma_start(w3_raw[:], w3.rearrange("(b p j) n -> p b j n", p=P, j=PACK))
-        quantize_w1((0, 1), 0, P)
-        quantize_w1((0, 1), P, 2 * P)
-        quantize_w1((0, 1), 2 * P, PASS)
-        def round_w1_in_pieces(key, first=0):
-            for m0 in range(first, P, 32):
+        cap_t[0] = load_rows(cap, 0, 0, M, keep, "late")
+        quantize_w1((0, 1), 0, 1, "w1_10")
+        quantize_w1((0, 1), 1, 2, "w1_codes01_b")
+        quantize_w1((0, 1), 2, PACK, "w1_codes01_c")
+        def round_w1_in_pieces(key):
+            for m0 in range(0, P, 32):
                 round_w1(nc.scalar.copy, key, slice(m0, m0 + 32))
 
         first_stage(0, 0, second_half_on_vector=True)
-        round_w1(nc.vector.tensor_copy, (1, 0), slice(0, P // 2))
         first_stage(0, 1)
-        round_w1_in_pieces((1, 0), P // 2)
-        cap_t[1] = load_rows(cap, 1, 0, M)
-        quantize_w1((1, 0), 0, PASS)
-        w2_codes = held([P, 2, 2 * N], U8, "w1_bf00")
+        round_w1_in_pieces((1, 0))
+        w3_raw = ring.tile([P, 2, PACK, N], F32, name="loaded", align_bytes=64)
+        nc.sync.dma_start(w3_raw[:], w3.rearrange("(b p j) n -> p b j n", p=P, j=PACK))
+        quantize_w1((1, 0), 0, PACK, "w1_codes10")
+        w2_codes = held([P, 2, 2 * N], U8, "w1_00")
         nc.sync.dma_start(w2_codes[:].bitcast(I32), w2_words.rearrange("a p c -> p a c").bitcast(I32))
-        w2_planes = held([P, 2, N], U8, "w1_bf01")
-        nc.gpsimd.memset(w2_planes[:].rearrange("p a c -> p (a c)").bitcast(I32), 0)
+        w2_planes = held([P, 2, N], U8, "w1_01")
+        nc.vector.memset(w2_planes[:].rearrange("p a c -> p (a c)").bitcast(I32), 0)
         w2_by_row = w2_scales.rearrange("a (d r) c -> r d a c", r=4)
         for r in range(4):
             nc.sync.dma_start(w2_planes[:].bitcast(I32)[r:P:32, :, :], w2_by_row[r].bitcast(I32))
-        bias_t = held([P, N // P], F32, "w1_bf10")
+        bias_t = held([P, N // P], F32, "w1_10")
         with nc.allow_non_contiguous_dma(reason="one bias value for each partition"):
             nc.sync.dma_start(bias_t[:], bias.rearrange("(c p) -> p c", p=P))
         first_stage(0, 2)
         round_w1_in_pieces((1, 1))
-        quantize_w1((1, 1), 0, PASS)
+        cap_t[1] = load_rows(cap, 1, 0, M)
+        quantize_w1((1, 1), 0, PACK, "w1_codes11")
         first_stage(0, 3)
         for t in range(PACK):
             subtract_pairs(0, t)

@@ -21,7 +21,8 @@ PACK = 4
 PASS = P * PACK
 BANK = 512
 HALF = M // 2
-VECTOR_SHARE = 64
+SPLIT_FIRST = 88
+SPLIT_LAST = 84
 
 
 def tile_list_signature_skew_features_kernel(
@@ -70,7 +71,10 @@ def tile_list_signature_skew_features_kernel(
         load_tab(0, keep, "first")
         w1_raw[0, 0] = load_rows(w1, 0, 0, PASS)
         load_tab(1, ring, "loaded")
-        w1_raw[0, 1] = load_rows(w1, 1, 0, PASS, keep, "late")
+        last_raw = [
+            load_rows(w1, 1, 0, PASS // 2, keep, "late_a"),
+            load_rows(w1, 1, PASS // 2, PASS, keep, "late"),
+        ]
 
 
         v_words = [held([P, S], U32, f"v_words{a}") for a in range(2)]
@@ -84,19 +88,20 @@ def tile_list_signature_skew_features_kernel(
         nc.vector.tensor_copy(v_planes[:].bitcast(I32), picked_rows[:].bitcast(I32))
         for a in range(2):
             for r in range(2):
-                nc.sync.dma_start(
+                nc.scalar.dma_start(
                     v_planes[:].bitcast(I32)[8 * a + 2 + r : P : 32, :],
                     picked_rows[:].bitcast(I32)[16 + 8 * a + r : P : 32, :],
                 )
 
         w1_bf, w1_codes, w1_planes = {}, {}, {}
 
-        def round_w1(copy, key, ms):
+        def round_w1(copy, key, lo, hi, raw=None, raw_lo=0):
             if key not in w1_bf:
                 w1_bf[key] = held([P, PACK, P, PACK], BF16, f"w1_{key[0]}{key[1]}")
+            raw = w1_raw[key] if raw is None else raw
             copy(
-                w1_bf[key][:, :, ms, :].rearrange("p t m j -> p m j t"),
-                w1_raw[key][:].rearrange("p j (m t) -> p m j t", t=PACK)[:, ms, :, :],
+                w1_bf[key][:, :, lo:hi, :].rearrange("p t m j -> p m j t"),
+                raw[:].rearrange("p j (m t) -> p m j t", t=PACK)[:, lo - raw_lo : hi - raw_lo, :, :],
             )
 
         def quantize(codes, planes, rounded, lo, hi):
@@ -229,22 +234,23 @@ def tile_list_signature_skew_features_kernel(
                 nc.scalar.activation(result[:, c, :], y[half, c][:], ACT.Sin, bias=bias_t[:, c : c + 1])
                 nc.sync.dma_start(out_rows[:, c, cols], result[:, c, :])
 
-        whole = slice(0, P)
         pick_words(0)
-        round_w1(nc.scalar.copy, (0, 0), whole)
+        round_w1(nc.scalar.copy, (0, 0), 0, SPLIT_FIRST)
+        round_w1(nc.vector.tensor_copy, (0, 0), SPLIT_FIRST, P)
+        quantize_w1((0, 0), 0, PACK, "w1_codes00")
         w1_raw[1, 0] = load_rows(w1, 0, PASS, 2 * PASS)
         pick_words(1)
         w1_raw[1, 1] = load_rows(w1, 1, PASS, 2 * PASS)
-        quantize_w1((0, 0), 0, PACK, "w1_codes00")
-        round_w1(nc.vector.tensor_copy, (0, 1), slice(0, VECTOR_SHARE))
-        round_w1(nc.scalar.copy, (0, 1), slice(VECTOR_SHARE, P))
+        round_w1(nc.scalar.copy, (0, 1), 0, P // 2, last_raw[0])
+        round_w1(nc.scalar.copy, (0, 1), P // 2, SPLIT_LAST, last_raw[1], P // 2)
+        round_w1(nc.vector.tensor_copy, (0, 1), SPLIT_LAST, P, last_raw[1], P // 2)
         cap_t[0] = load_rows(cap, 0, 0, M, keep, "late")
         quantize_w1((0, 1), 0, 1, "w1_10")
         quantize_w1((0, 1), 1, 2, "w1_codes01_b")
         quantize_w1((0, 1), 2, PACK, "w1_codes01_c")
         def round_w1_in_pieces(key):
             for m0 in range(0, P, 32):
-                round_w1(nc.scalar.copy, key, slice(m0, m0 + 32))
+                round_w1(nc.scalar.copy, key, m0, m0 + 32)
 
         first_stage(0, 0, second_half_on_vector=True)
         first_stage(0, 1)

@@ -20,9 +20,12 @@ P = 128
 PACK = 4
 PASS = P * PACK
 BANK = 512
+GROUP = 16
 HALF = M // 2
-SPLIT_FIRST = 88
+SPLIT_FIRST = 82
 SPLIT_LAST = 84
+PIECE = 32
+EARLY_TILES = 2
 
 
 def tile_list_signature_skew_features_kernel(
@@ -34,12 +37,15 @@ def tile_list_signature_skew_features_kernel(
         ring = ctx.enter_context(tc.tile_pool(name="ring", bufs=2))
         psum = ctx.enter_context(tc.psum_pool(name="psum", bufs=1))
 
-        def held(shape, dtype, name):
-            return keep.tile(shape, dtype, name=name, align_bytes=64)
+        def held(shape, dtype, name, tag=""):
+            return keep.tile(shape, dtype, name=name, tag=tag, align_bytes=64)
 
-        offs_t = keep.tile([P, S // 16], U16, name="offs_t")
-        pos1_t = keep.tile([P, M // 16], U16, name="pos1_t")
-        pos2_t = keep.tile([P, M // 16], U16, name="pos2_t")
+        def streamed(shape, dtype, name):
+            return ring.tile(shape, dtype, name=name, tag="streamed", align_bytes=64)
+
+        offs_t = keep.tile([P, S // GROUP], U16, name="offs_t")
+        pos1_t = keep.tile([P, M // GROUP], U16, name="pos1_t")
+        pos2_t = keep.tile([P, M // GROUP], U16, name="pos2_t")
         nc.sync.dma_start(offs_t[:], offs)
         nc.sync.dma_start(pos1_t[:], pos1)
         nc.sync.dma_start(pos2_t[:], pos2)
@@ -48,34 +54,29 @@ def tile_list_signature_skew_features_kernel(
 
         tab_rows = held([P, T], U8, "tab_rows")
         nc.gpsimd.memset(tab_rows[:].bitcast(I32), 0)
-        by_row = tab_scales.rearrange("a (g r) t -> r g a t", r=2)
+        tab_by_row = tab_scales.rearrange("a (g r) t -> r g a t", r=2)
         for r in range(2):
-            nc.sync.dma_start(tab_rows[:].bitcast(I32)[r:P:8, :], by_row[r].bitcast(I32))
+            nc.sync.dma_start(tab_rows[:].bitcast(I32)[r:P:8, :], tab_by_row[r].bitcast(I32))
 
         zero_in = held([P, 1], F32, "zero_in")
         zero = held([P, 1], F32, "zero")
         nc.gpsimd.memset(zero_in[:], 0.0)
         nc.scalar.activation(zero[:], zero_in[:], ACT.Sin)
 
-        tab, w1_raw, cap_t = {}, {}, {}
+        def load_words(dst, a):
+            nc.sync.dma_start(dst[:], tab_words[a].rearrange("p t i -> p (t i)").bitcast(I32))
+            return dst
 
-        def load_tab(a, pool, name):
-            tab[a] = pool.tile([P, T], I32, name=name, align_bytes=64)
-            nc.sync.dma_start(tab[a][:], tab_words[a].rearrange("p t i -> p (t i)").bitcast(I32))
-
-        def load_rows(src, a, lo, hi, pool=ring, name="loaded"):
-            dst = pool.tile([P, PACK, hi - lo], F32, name=name, align_bytes=64)
+        def load_rows(dst, src, a, lo, hi):
             nc.sync.dma_start(dst[:], src[a * PASS : (a + 1) * PASS, lo:hi].rearrange("(p j) c -> p j c", j=PACK))
             return dst
 
-        load_tab(0, keep, "first")
-        w1_raw[0, 0] = load_rows(w1, 0, 0, PASS)
-        load_tab(1, ring, "loaded")
-        last_raw = [
-            load_rows(w1, 1, 0, PASS // 2, keep, "late_a"),
-            load_rows(w1, 1, PASS // 2, PASS, keep, "late"),
-        ]
-
+        tab, w1_raw, cap_t = {}, {}, {}
+        tab[0] = load_words(held([P, T], I32, "tab0"), 0)
+        w1_raw[0, 0] = load_rows(streamed([P, PACK, PASS], F32, "w1_raw00"), w1, 0, 0, PASS)
+        tab[1] = load_words(streamed([P, T], I32, "tab1"), 1)
+        w1_left = load_rows(held([P, PACK, PASS // 2], F32, "w1_left"), w1, 1, 0, PASS // 2)
+        w1_right = load_rows(held([P, PACK, PASS // 2], F32, "w1_right", "w1_right"), w1, 1, PASS // 2, PASS)
 
         v_words = [held([P, S], U32, f"v_words{a}") for a in range(2)]
 
@@ -90,43 +91,42 @@ def tile_list_signature_skew_features_kernel(
             for r in range(2):
                 nc.scalar.dma_start(
                     v_planes[:].bitcast(I32)[8 * a + 2 + r : P : 32, :],
-                    picked_rows[:].bitcast(I32)[16 + 8 * a + r : P : 32, :],
+                    picked_rows[:].bitcast(I32)[GROUP + 8 * a + r : P : 32, :],
                 )
 
-        w1_bf, w1_codes, w1_planes = {}, {}, {}
+        w1_bf, w1_codes, w1_planes, h = {}, {}, {}, {}
 
-        def round_w1(copy, key, lo, hi, raw=None, raw_lo=0):
+        def round_w1(copy, key, raw, lo, hi, raw_lo=0):
             if key not in w1_bf:
-                w1_bf[key] = held([P, PACK, P, PACK], BF16, f"w1_{key[0]}{key[1]}")
-            raw = w1_raw[key] if raw is None else raw
+                w1_bf[key] = held([P, PACK, P, PACK], BF16, f"w1_bf{key[0]}{key[1]}", f"w1_bf{key[0]}{key[1]}")
             copy(
                 w1_bf[key][:, :, lo:hi, :].rearrange("p t m j -> p m j t"),
                 raw[:].rearrange("p j (m t) -> p m j t", t=PACK)[:, lo - raw_lo : hi - raw_lo, :, :],
             )
 
-        def quantize(codes, planes, rounded, lo, hi):
-            nc.vector.quantize_mx(
-                out=codes[:, lo:hi].bitcast(FP8X4), scales=planes[:, lo:hi], in_=rounded[:, PACK * lo : PACK * hi]
-            )
+        def round_w1_in_pieces(key):
+            for lo in range(0, P, PIECE):
+                round_w1(nc.scalar.copy, key, w1_raw[key], lo, lo + PIECE)
 
-        def quantize_w1(key, t_lo, t_hi, name):
+        def quantize(codes, planes, rounded):
+            nc.vector.quantize_mx(out=codes.bitcast(FP8X4), scales=planes, in_=rounded)
+
+        def quantize_w1(key, t_lo, t_hi, tag=""):
             width = (t_hi - t_lo) * P
-            codes = held([P, width], U32, name)
-            planes = held([P, width], U8, name + "_planes")
-            quantize(codes, planes, w1_bf[key][:, t_lo:t_hi].rearrange("p t m j -> p (t m j)"), 0, width)
+            codes = held([P, width], U32, f"w1_codes{key[0]}{key[1]}{t_lo}", tag)
+            planes = held([P, width], U8, f"w1_planes{key[0]}{key[1]}{t_lo}")
+            quantize(codes[:], planes[:], w1_bf[key][:, t_lo:t_hi].rearrange("p t m j -> p (t m j)"))
             for t in range(t_lo, t_hi):
                 cols = slice((t - t_lo) * P, (t - t_lo + 1) * P)
                 w1_codes[key + (t,)] = codes[:, cols]
                 w1_planes[key + (t,)] = planes[:, cols]
 
-        h = {}
-
-        def first_stage(b, t, second_half_on_vector=False):
+        def first_stage(b, t, last_copy_on_vector=False):
             h[b, t] = held([P, S], F32, f"h{b}{t}")
+            passes = (0, 1) if t < EARLY_TILES else (1, 0)
             for u in range(S // BANK):
-                acc = psum.tile([P, BANK], F32, name=f"bank{(2 * t + u) % 8}")
+                acc = psum.tile([P, BANK], F32, name=f"bank{2 * t + u}")
                 picked = slice(u * BANK, (u + 1) * BANK)
-                passes = (0, 1) if t == 0 else (1, 0)
                 for a in passes:
                     nc.tensor.matmul_mx(
                         acc[:],
@@ -137,36 +137,34 @@ def tile_list_signature_skew_features_kernel(
                         start=(a == passes[0]),
                         stop=(a == passes[1]),
                     )
-                if u == 1 and second_half_on_vector:
+                if u == 1 and last_copy_on_vector:
                     nc.vector.tensor_scalar_mul(h[b, t][:, picked], acc[:], gain_t[:, b, t : t + 1])
                 else:
                     nc.scalar.activation(h[b, t][:, picked], acc[:], ACT.Copy, scale=gain_t[:, b, t : t + 1])
 
-        units = [(b, lo, lo + HALF) for b in range(2) for lo in (0, HALF)]
-        signed = {u: held([P, PACK, u[2] - u[1]], F32, f"signed{i}") for i, u in enumerate(units)}
-        dif = {u: held([P, PACK, u[2] - u[1]], F32, f"dif{i}") for i, u in enumerate(units)}
-        dif_bf = {u: held([P, u[2] - u[1], PACK], BF16, f"dif_bf{i}") for i, u in enumerate(units)}
-        low_bf = {u: held([P, u[2] - u[1], PACK], BF16, f"low_bf{i}") for i, u in enumerate(units)}
+        units = [(b, half) for b in range(2) for half in range(2)]
+        signed = {u: held([P, PACK, HALF], F32, f"signed{u[0]}{u[1]}") for u in units}
+        dif = {u: held([P, PACK, HALF], F32, f"dif{u[0]}{u[1]}") for u in units}
+        dif_bf = {u: held([P, HALF, PACK], BF16, f"dif_bf{u[0]}{u[1]}") for u in units}
+        low_bf = {u: held([P, HALF, PACK], BF16, f"low_bf{u[0]}{u[1]}") for u in units}
         dif_codes = [held([P, M], U32, f"dif_codes{b}") for b in range(2)]
         low_codes = [held([P, M], U32, f"low_codes{b}") for b in range(2)]
         dif_planes = [held([P, M], U8, f"dif_planes{b}") for b in range(2)]
         low_planes = [held([P, M], U8, f"low_planes{b}") for b in range(2)]
 
-        def subtract_pairs(b, t):
-            second = {}
-            for u in units[2 * b : 2 * b + 2]:
-                second[u] = ring.tile([P, HALF], F32, name="second", bufs=4)
-                nc.vector.tensor_copy(second[u][:], h[b, t][:].indirect(pos2_t[:, u[1] // 16 : u[2] // 16]))
-            for u in units[2 * b : 2 * b + 2]:
-                nc.vector.tensor_tensor(
-                    signed[u][:, t, :],
-                    h[b, t][:].indirect(pos1_t[:, u[1] // 16 : u[2] // 16]),
-                    second[u][:],
-                    ALU.subtract,
-                )
+        def out_cols(half):
+            return slice(half * HALF, (half + 1) * HALF)
 
-        def take_abs(u, t):
-            nc.scalar.activation(dif[u][:, t, :], signed[u][:, t, :], ACT.Abs, bias=zero[:])
+        def subtract_pairs(b, t):
+            second, lists = {}, {}
+            for half in range(2):
+                lists[half] = slice(half * HALF // GROUP, (half + 1) * HALF // GROUP)
+                second[half] = ring.tile([P, HALF], F32, name="second", bufs=4)
+                nc.vector.tensor_copy(second[half][:], h[b, t][:].indirect(pos2_t[:, lists[half]]))
+            for half in range(2):
+                nc.vector.tensor_tensor(
+                    signed[b, half][:, t, :], h[b, t][:].indirect(pos1_t[:, lists[half]]), second[half][:], ALU.subtract
+                )
 
         def pairs_in(rows):
             return rows.rearrange("p t (c i) -> p c t i", i=2)
@@ -174,27 +172,28 @@ def tile_list_signature_skew_features_kernel(
         def pairs_out(words):
             return words.rearrange("p (c i) t -> p c t i", i=2)
 
+        def take_abs(u, t):
+            nc.scalar.activation(dif[u][:, t, :], signed[u][:, t, :], ACT.Abs, bias=zero[:])
+
         def round_dif(u):
             nc.scalar.activation(pairs_out(dif_bf[u][:]), pairs_in(signed[u][:]), ACT.Abs, bias=zero[:])
 
         def round_low(u):
-            b, lo, hi = u
-            nc.vector.tensor_tensor(pairs_out(low_bf[u][:]), pairs_in(dif[u][:]), pairs_in(cap_t[b][:, :, lo:hi]), ALU.min)
+            caps = cap_t[u[0]][:, :, out_cols(u[1])]
+            nc.vector.tensor_tensor(pairs_out(low_bf[u][:]), pairs_in(dif[u][:]), pairs_in(caps), ALU.min)
 
         def quantize_unit(codes, planes, rounded, u):
-            b, lo, hi = u
-            quantize(codes[b][:, lo:hi], planes[b][:, lo:hi], rounded[u][:].rearrange("p m t -> p (m t)"), 0, hi - lo)
+            cols = out_cols(u[1])
+            quantize(codes[u[0]][:, cols], planes[u[0]][:, cols], rounded[u][:].rearrange("p m t -> p (m t)"))
 
         w3_bf = held([P, 2, N, PACK], BF16, "w3_bf")
         w3_codes = held([P, 2 * N], U32, "w3_codes")
         w3_planes = held([P, 2 * N], U8, "w3_planes")
-
         y = {}
 
         def second_stage(b, half, c):
-            lo = half * HALF
             if b == 0:
-                y[half, c] = psum.tile([P, HALF], F32, name=f"bank{3 * half + c}")
+                y[half, c] = psum.tile([P, HALF], F32, name=f"bank{N // P * half + c}")
             acc = y[half, c]
 
             def low_pass():
@@ -203,8 +202,8 @@ def tile_list_signature_skew_features_kernel(
                     acc[:],
                     lhsT=w3_codes[:, w3_cols].bitcast(FP8X4),
                     lhsT_scale=w3_planes[:, w3_cols],
-                    rhs=low_codes[b][:, lo : lo + HALF].bitcast(FP8X4),
-                    rhs_scale=low_planes[b][:, lo : lo + HALF],
+                    rhs=low_codes[b][:, out_cols(half)].bitcast(FP8X4),
+                    rhs_scale=low_planes[b][:, out_cols(half)],
                     start=(b == 0),
                     stop=(b == 1),
                 )
@@ -212,12 +211,13 @@ def tile_list_signature_skew_features_kernel(
             if b == 0:
                 low_pass()
             for m0 in range(0, HALF, P):
+                dif_cols = slice(half * HALF + m0, half * HALF + m0 + P)
                 nc.tensor.matmul_mx(
                     acc[:, m0 : m0 + P],
                     lhsT=w2_codes[:, b, 2 * c * P : 2 * (c + 1) * P].bitcast(FP4X4),
                     lhsT_scale=w2_planes[:, b, c * P : (c + 1) * P],
-                    rhs=dif_codes[b][:, lo + m0 : lo + m0 + P].bitcast(FP8X4),
-                    rhs_scale=dif_planes[b][:, lo + m0 : lo + m0 + P],
+                    rhs=dif_codes[b][:, dif_cols].bitcast(FP8X4),
+                    rhs_scale=dif_planes[b][:, dif_cols],
                     start=False,
                     stop=False,
                 )
@@ -228,55 +228,55 @@ def tile_list_signature_skew_features_kernel(
 
         def finish(half):
             result = held([P, N // P, HALF], F32, f"result{half}")
-            cols = slice(half * HALF, (half + 1) * HALF)
             for c in range(N // P):
                 second_stage(1, half, c)
                 nc.scalar.activation(result[:, c, :], y[half, c][:], ACT.Sin, bias=bias_t[:, c : c + 1])
-                nc.sync.dma_start(out_rows[:, c, cols], result[:, c, :])
+                nc.sync.dma_start(out_rows[:, c, out_cols(half)], result[:, c, :])
 
         pick_words(0)
-        round_w1(nc.scalar.copy, (0, 0), 0, SPLIT_FIRST)
-        round_w1(nc.vector.tensor_copy, (0, 0), SPLIT_FIRST, P)
-        quantize_w1((0, 0), 0, PACK, "w1_codes00")
-        w1_raw[1, 0] = load_rows(w1, 0, PASS, 2 * PASS)
+        round_w1(nc.scalar.copy, (0, 0), w1_raw[0, 0], 0, SPLIT_FIRST)
+        round_w1(nc.vector.tensor_copy, (0, 0), w1_raw[0, 0], SPLIT_FIRST, P)
+        quantize_w1((0, 0), 0, PACK)
+        w1_raw[1, 0] = load_rows(streamed([P, PACK, PASS], F32, "w1_raw10"), w1, 0, PASS, 2 * PASS)
         pick_words(1)
-        w1_raw[1, 1] = load_rows(w1, 1, PASS, 2 * PASS)
-        round_w1(nc.scalar.copy, (0, 1), 0, P // 2, last_raw[0])
-        round_w1(nc.scalar.copy, (0, 1), P // 2, SPLIT_LAST, last_raw[1], P // 2)
-        round_w1(nc.vector.tensor_copy, (0, 1), SPLIT_LAST, P, last_raw[1], P // 2)
-        cap_t[0] = load_rows(cap, 0, 0, M, keep, "late")
-        quantize_w1((0, 1), 0, 1, "w1_10")
-        quantize_w1((0, 1), 1, 2, "w1_codes01_b")
-        quantize_w1((0, 1), 2, PACK, "w1_codes01_c")
-        def round_w1_in_pieces(key):
-            for m0 in range(0, P, 32):
-                round_w1(nc.scalar.copy, key, m0, m0 + 32)
+        w1_raw[1, 1] = load_rows(streamed([P, PACK, PASS], F32, "w1_raw11"), w1, 1, PASS, 2 * PASS)
+        round_w1(nc.scalar.copy, (0, 1), w1_left, 0, P // 2)
+        round_w1(nc.scalar.copy, (0, 1), w1_right, P // 2, SPLIT_LAST, P // 2)
+        round_w1(nc.vector.tensor_copy, (0, 1), w1_right, SPLIT_LAST, P, P // 2)
+        cap_t[0] = load_rows(held([P, PACK, M], F32, "cap0", "w1_right"), cap, 0, 0, M)
+        quantize_w1((0, 1), 0, 1, "w1_bf10")
+        quantize_w1((0, 1), 1, 2)
+        quantize_w1((0, 1), 2, PACK)
 
-        first_stage(0, 0, second_half_on_vector=True)
+        first_stage(0, 0, last_copy_on_vector=True)
         first_stage(0, 1)
         round_w1_in_pieces((1, 0))
-        w3_raw = ring.tile([P, 2, PACK, N], F32, name="loaded", align_bytes=64)
+        w3_raw = streamed([P, 2, PACK, N], F32, "w3_raw")
         nc.sync.dma_start(w3_raw[:], w3.rearrange("(b p j) n -> p b j n", p=P, j=PACK))
-        quantize_w1((1, 0), 0, PACK, "w1_codes10")
-        w2_codes = held([P, 2, 2 * N], U8, "w1_00")
+        quantize_w1((1, 0), 0, PACK)
+
+        w2_codes = held([P, 2, 2 * N], U8, "w2_codes", "w1_bf00")
         nc.sync.dma_start(w2_codes[:].bitcast(I32), w2_words.rearrange("a p c -> p a c").bitcast(I32))
-        w2_planes = held([P, 2, N], U8, "w1_01")
+        w2_planes = held([P, 2, N], U8, "w2_planes", "w1_bf01")
         nc.vector.memset(w2_planes[:].rearrange("p a c -> p (a c)").bitcast(I32), 0)
-        w2_by_row = w2_scales.rearrange("a (d r) c -> r d a c", r=4)
-        for r in range(4):
-            nc.sync.dma_start(w2_planes[:].bitcast(I32)[r:P:32, :, :], w2_by_row[r].bitcast(I32))
-        bias_t = held([P, N // P], F32, "w1_10")
+        w2_by_row = w2_scales.rearrange("a (d i) c -> i d a c", i=4)
+        for i in range(4):
+            nc.sync.dma_start(w2_planes[:].bitcast(I32)[i:P:32, :, :], w2_by_row[i].bitcast(I32))
+        bias_t = held([P, N // P], F32, "bias_t", "w1_bf10")
         with nc.allow_non_contiguous_dma(reason="one bias value for each partition"):
             nc.sync.dma_start(bias_t[:], bias.rearrange("(c p) -> p c", p=P))
+
         first_stage(0, 2)
         round_w1_in_pieces((1, 1))
-        cap_t[1] = load_rows(cap, 1, 0, M)
-        quantize_w1((1, 1), 0, PACK, "w1_codes11")
+        cap_t[1] = load_rows(streamed([P, PACK, M], F32, "cap1"), cap, 1, 0, M)
+        quantize_w1((1, 1), 0, PACK)
         first_stage(0, 3)
         for t in range(PACK):
             subtract_pairs(0, t)
-        first_stage(1, 0)
+
         for t in range(PACK):
+            if t == PACK // 2:
+                first_stage(1, 0)
             for u in units[:2]:
                 take_abs(u, t)
         first_stage(1, 1)
@@ -285,18 +285,19 @@ def tile_list_signature_skew_features_kernel(
         for u in units[:2]:
             round_dif(u)
         first_stage(1, 2)
-        nc.scalar.copy(pairs_out(w3_bf[:, 0, :, :]), pairs_in(w3_raw[:, 0, :, :]))
-        nc.scalar.copy(pairs_out(w3_bf[:, 1, :, :]), pairs_in(w3_raw[:, 1, :, :]))
+        for b in range(2):
+            nc.scalar.copy(pairs_out(w3_bf[:, b, :, :]), pairs_in(w3_raw[:, b, :, :]))
         first_stage(1, 3)
         w3_flat = w3_bf[:].rearrange("p b n j -> p (b n j)")
-        quantize(w3_codes, w3_planes, w3_flat, 0, PASS)
-        quantize(w3_codes, w3_planes, w3_flat, PASS, 2 * N)
+        for lo, hi in ((0, PASS), (PASS, 2 * N)):
+            quantize(w3_codes[:, lo:hi], w3_planes[:, lo:hi], w3_flat[:, PACK * lo : PACK * hi])
         for u in units[:2]:
             quantize_unit(low_codes, low_planes, low_bf, u)
             quantize_unit(dif_codes, dif_planes, dif_bf, u)
         for half in range(2):
             for c in range(N // P):
                 second_stage(0, half, c)
+
         for t in range(PACK):
             subtract_pairs(1, t)
         for t in range(PACK - 1):
@@ -305,8 +306,7 @@ def tile_list_signature_skew_features_kernel(
         for u in units[2:]:
             take_abs(u, PACK - 1)
             round_dif(u)
-        for half in range(2):
-            u = units[2 + half]
+        for u in units[2:]:
             round_low(u)
             quantize_unit(dif_codes, dif_planes, dif_bf, u)
             quantize_unit(low_codes, low_planes, low_bf, u)

from contextlib import ExitStack

import concourse.mybir as mybir

K, T, S, M, H, N = 1024, 2048, 1024, 512, 1024, 384
FLOPS = 2 * K * H * S + 2 * 2 * H * N * M

F32 = mybir.dt.float32
BF16 = mybir.dt.bfloat16
I32 = mybir.dt.int32
U32 = mybir.dt.uint32
U16 = mybir.dt.uint16
U8 = mybir.dt.uint8
FP8X4 = mybir.dt.float8_e4m3fn_x4
FP4X4 = mybir.dt.float4_e2m1fn_x4
ALU = mybir.AluOpType
ACT = mybir.ActivationFunctionType

P = 128
PACK = 4
PASS = P * PACK
BANK = 512
GROUP = 16
HALF = M // 2
SPLIT_FIRST = 82
SPLIT_LAST = 84
PIECE = 32
EARLY_TILES = 2


def tile_list_signature_skew_features_kernel(
    tc, tab_words, tab_scales, offs, pos1, pos2, w1, gain, cap, w2_words, w2_scales, w3, bias, out
):
    nc = tc.nc
    with ExitStack() as ctx:
        keep = ctx.enter_context(tc.tile_pool(name="keep", bufs=1))
        ring = ctx.enter_context(tc.tile_pool(name="ring", bufs=2))
        psum = ctx.enter_context(tc.psum_pool(name="psum", bufs=1))

        def held(shape, dtype, name, tag=""):
            return keep.tile(shape, dtype, name=name, tag=tag, align_bytes=64)

        def streamed(shape, dtype, name):
            return ring.tile(shape, dtype, name=name, tag="streamed", align_bytes=64)

        offs_t = keep.tile([P, S // GROUP], U16, name="offs_t")
        pos1_t = keep.tile([P, M // GROUP], U16, name="pos1_t")
        pos2_t = keep.tile([P, M // GROUP], U16, name="pos2_t")
        nc.sync.dma_start(offs_t[:], offs)
        nc.sync.dma_start(pos1_t[:], pos1)
        nc.sync.dma_start(pos2_t[:], pos2)
        gain_t = held([P, 2, PACK], F32, "gain_t")
        nc.sync.dma_start(gain_t[:], gain.rearrange("(b p t) -> p b t", p=P, t=PACK))

        tab_rows = held([P, T], U8, "tab_rows")
        nc.gpsimd.memset(tab_rows[:].bitcast(I32), 0)
        tab_by_row = tab_scales.rearrange("a (g r) t -> r g a t", r=2)
        for r in range(2):
            nc.sync.dma_start(tab_rows[:].bitcast(I32)[r:P:8, :], tab_by_row[r].bitcast(I32))

        zero_in = held([P, 1], F32, "zero_in")
        zero = held([P, 1], F32, "zero")
        nc.gpsimd.memset(zero_in[:], 0.0)
        nc.scalar.activation(zero[:], zero_in[:], ACT.Sin)

        def load_words(dst, a):
            nc.sync.dma_start(dst[:], tab_words[a].rearrange("p t i -> p (t i)").bitcast(I32))
            return dst

        def load_rows(dst, src, a, lo, hi):
            nc.sync.dma_start(dst[:], src[a * PASS : (a + 1) * PASS, lo:hi].rearrange("(p j) c -> p j c", j=PACK))
            return dst

        tab, w1_raw, cap_t = {}, {}, {}
        tab[0] = load_words(held([P, T], I32, "tab0"), 0)
        w1_raw[0, 0] = load_rows(streamed([P, PACK, PASS], F32, "w1_raw00"), w1, 0, 0, PASS)
        tab[1] = load_words(streamed([P, T], I32, "tab1"), 1)
        w1_left = load_rows(held([P, PACK, PASS // 2], F32, "w1_left"), w1, 1, 0, PASS // 2)
        w1_right = load_rows(held([P, PACK, PASS // 2], F32, "w1_right", "w1_right"), w1, 1, PASS // 2, PASS)

        v_words = [held([P, S], U32, f"v_words{a}") for a in range(2)]

        def pick_words(a):
            nc.vector.tensor_copy(v_words[a][:], tab[a][:].bitcast(U32).indirect(offs_t[:]))

        picked_rows = held([P, S], U8, "picked_rows")
        nc.vector.tensor_copy(picked_rows[:], tab_rows[:].indirect(offs_t[:]))
        v_planes = held([P, S], U8, "v_planes")
        nc.vector.tensor_copy(v_planes[:].bitcast(I32), picked_rows[:].bitcast(I32))
        for a in range(2):
            for r in range(2):
                nc.scalar.dma_start(
                    v_planes[:].bitcast(I32)[8 * a + 2 + r : P : 32, :],
                    picked_rows[:].bitcast(I32)[GROUP + 8 * a + r : P : 32, :],
                )

        w1_bf, w1_codes, w1_planes, h = {}, {}, {}, {}

        def round_w1(copy, key, raw, lo, hi, raw_lo=0):
            if key not in w1_bf:
                w1_bf[key] = held([P, PACK, P, PACK], BF16, f"w1_bf{key[0]}{key[1]}", f"w1_bf{key[0]}{key[1]}")
            copy(
                w1_bf[key][:, :, lo:hi, :].rearrange("p t m j -> p m j t"),
                raw[:].rearrange("p j (m t) -> p m j t", t=PACK)[:, lo - raw_lo : hi - raw_lo, :, :],
            )

        def round_w1_in_pieces(key):
            for lo in range(0, P, PIECE):
                round_w1(nc.scalar.copy, key, w1_raw[key], lo, lo + PIECE)

        def quantize(codes, planes, rounded):
            nc.vector.quantize_mx(out=codes.bitcast(FP8X4), scales=planes, in_=rounded)

        def quantize_w1(key, t_lo, t_hi, tag=""):
            width = (t_hi - t_lo) * P
            codes = held([P, width], U32, f"w1_codes{key[0]}{key[1]}{t_lo}", tag)
            planes = held([P, width], U8, f"w1_planes{key[0]}{key[1]}{t_lo}")
            quantize(codes[:], planes[:], w1_bf[key][:, t_lo:t_hi].rearrange("p t m j -> p (t m j)"))
            for t in range(t_lo, t_hi):
                cols = slice((t - t_lo) * P, (t - t_lo + 1) * P)
                w1_codes[key + (t,)] = codes[:, cols]
                w1_planes[key + (t,)] = planes[:, cols]

        def first_stage(b, t, last_copy_on_vector=False):
            h[b, t] = held([P, S], F32, f"h{b}{t}")
            passes = (0, 1) if t < EARLY_TILES else (1, 0)
            for u in range(S // BANK):
                acc = psum.tile([P, BANK], F32, name=f"bank{2 * t + u}")
                picked = slice(u * BANK, (u + 1) * BANK)
                for a in passes:
                    nc.tensor.matmul_mx(
                        acc[:],
                        lhsT=w1_codes[b, a, t].bitcast(FP8X4),
                        lhsT_scale=w1_planes[b, a, t],
                        rhs=v_words[a][:, picked].bitcast(FP8X4),
                        rhs_scale=v_planes[8 * a : P, picked],
                        start=(a == passes[0]),
                        stop=(a == passes[1]),
                    )
                if u == 1 and last_copy_on_vector:
                    nc.vector.tensor_scalar_mul(h[b, t][:, picked], acc[:], gain_t[:, b, t : t + 1])
                else:
                    nc.scalar.activation(h[b, t][:, picked], acc[:], ACT.Copy, scale=gain_t[:, b, t : t + 1])

        units = [(b, half) for b in range(2) for half in range(2)]
        signed = {u: held([P, PACK, HALF], F32, f"signed{u[0]}{u[1]}") for u in units}
        dif = {u: held([P, PACK, HALF], F32, f"dif{u[0]}{u[1]}") for u in units}
        dif_bf = {u: held([P, HALF, PACK], BF16, f"dif_bf{u[0]}{u[1]}") for u in units}
        low_bf = {u: held([P, HALF, PACK], BF16, f"low_bf{u[0]}{u[1]}") for u in units}
        dif_codes = [held([P, M], U32, f"dif_codes{b}") for b in range(2)]
        low_codes = [held([P, M], U32, f"low_codes{b}") for b in range(2)]
        dif_planes = [held([P, M], U8, f"dif_planes{b}") for b in range(2)]
        low_planes = [held([P, M], U8, f"low_planes{b}") for b in range(2)]

        def out_cols(half):
            return slice(half * HALF, (half + 1) * HALF)

        def subtract_pairs(b, t):
            second, lists = {}, {}
            for half in range(2):
                lists[half] = slice(half * HALF // GROUP, (half + 1) * HALF // GROUP)
                second[half] = ring.tile([P, HALF], F32, name="second", bufs=4)
                nc.vector.tensor_copy(second[half][:], h[b, t][:].indirect(pos2_t[:, lists[half]]))
            for half in range(2):
                nc.vector.tensor_tensor(
                    signed[b, half][:, t, :], h[b, t][:].indirect(pos1_t[:, lists[half]]), second[half][:], ALU.subtract
                )

        def pairs_in(rows):
            return rows.rearrange("p t (c i) -> p c t i", i=2)

        def pairs_out(words):
            return words.rearrange("p (c i) t -> p c t i", i=2)

        def take_abs(u, t):
            nc.scalar.activation(dif[u][:, t, :], signed[u][:, t, :], ACT.Abs, bias=zero[:])

        def round_dif(u):
            nc.scalar.activation(pairs_out(dif_bf[u][:]), pairs_in(signed[u][:]), ACT.Abs, bias=zero[:])

        def round_low(u):
            caps = cap_t[u[0]][:, :, out_cols(u[1])]
            nc.vector.tensor_tensor(pairs_out(low_bf[u][:]), pairs_in(dif[u][:]), pairs_in(caps), ALU.min)

        def quantize_unit(codes, planes, rounded, u):
            cols = out_cols(u[1])
            quantize(codes[u[0]][:, cols], planes[u[0]][:, cols], rounded[u][:].rearrange("p m t -> p (m t)"))

        w3_bf = held([P, 2, N, PACK], BF16, "w3_bf")
        w3_codes = held([P, 2 * N], U32, "w3_codes")
        w3_planes = held([P, 2 * N], U8, "w3_planes")
        y = {}

        def second_stage(b, half, c):
            if b == 0:
                y[half, c] = psum.tile([P, HALF], F32, name=f"bank{N // P * half + c}")
            acc = y[half, c]

            def low_pass():
                w3_cols = slice(b * N + c * P, b * N + (c + 1) * P)
                nc.tensor.matmul_mx(
                    acc[:],
                    lhsT=w3_codes[:, w3_cols].bitcast(FP8X4),
                    lhsT_scale=w3_planes[:, w3_cols],
                    rhs=low_codes[b][:, out_cols(half)].bitcast(FP8X4),
                    rhs_scale=low_planes[b][:, out_cols(half)],
                    start=(b == 0),
                    stop=(b == 1),
                )

            if b == 0:
                low_pass()
            for m0 in range(0, HALF, P):
                dif_cols = slice(half * HALF + m0, half * HALF + m0 + P)
                nc.tensor.matmul_mx(
                    acc[:, m0 : m0 + P],
                    lhsT=w2_codes[:, b, 2 * c * P : 2 * (c + 1) * P].bitcast(FP4X4),
                    lhsT_scale=w2_planes[:, b, c * P : (c + 1) * P],
                    rhs=dif_codes[b][:, dif_cols].bitcast(FP8X4),
                    rhs_scale=dif_planes[b][:, dif_cols],
                    start=False,
                    stop=False,
                )
            if b == 1:
                low_pass()

        out_rows = out.rearrange("(c p) m -> p c m", p=P)

        def finish(half):
            result = held([P, N // P, HALF], F32, f"result{half}")
            for c in range(N // P):
                second_stage(1, half, c)
                nc.scalar.activation(result[:, c, :], y[half, c][:], ACT.Sin, bias=bias_t[:, c : c + 1])
                nc.sync.dma_start(out_rows[:, c, out_cols(half)], result[:, c, :])

        pick_words(0)
        round_w1(nc.scalar.copy, (0, 0), w1_raw[0, 0], 0, SPLIT_FIRST)
        round_w1(nc.vector.tensor_copy, (0, 0), w1_raw[0, 0], SPLIT_FIRST, P)
        quantize_w1((0, 0), 0, PACK)
        w1_raw[1, 0] = load_rows(streamed([P, PACK, PASS], F32, "w1_raw10"), w1, 0, PASS, 2 * PASS)
        pick_words(1)
        w1_raw[1, 1] = load_rows(streamed([P, PACK, PASS], F32, "w1_raw11"), w1, 1, PASS, 2 * PASS)
        round_w1(nc.scalar.copy, (0, 1), w1_left, 0, P // 2)
        round_w1(nc.scalar.copy, (0, 1), w1_right, P // 2, SPLIT_LAST, P // 2)
        round_w1(nc.vector.tensor_copy, (0, 1), w1_right, SPLIT_LAST, P, P // 2)
        cap_t[0] = load_rows(held([P, PACK, M], F32, "cap0", "w1_right"), cap, 0, 0, M)
        quantize_w1((0, 1), 0, 1, "w1_bf10")
        quantize_w1((0, 1), 1, 2)
        quantize_w1((0, 1), 2, PACK)

        first_stage(0, 0, last_copy_on_vector=True)
        first_stage(0, 1)
        round_w1_in_pieces((1, 0))
        w3_raw = streamed([P, 2, PACK, N], F32, "w3_raw")
        nc.sync.dma_start(w3_raw[:], w3.rearrange("(b p j) n -> p b j n", p=P, j=PACK))
        quantize_w1((1, 0), 0, PACK)

        w2_codes = held([P, 2, 2 * N], U8, "w2_codes", "w1_bf00")
        nc.sync.dma_start(w2_codes[:].bitcast(I32), w2_words.rearrange("a p c -> p a c").bitcast(I32))
        w2_planes = held([P, 2, N], U8, "w2_planes", "w1_bf01")
        nc.vector.memset(w2_planes[:].rearrange("p a c -> p (a c)").bitcast(I32), 0)
        w2_by_row = w2_scales.rearrange("a (d i) c -> i d a c", i=4)
        for i in range(4):
            nc.sync.dma_start(w2_planes[:].bitcast(I32)[i:P:32, :, :], w2_by_row[i].bitcast(I32))
        bias_t = held([P, N // P], F32, "bias_t", "w1_bf10")
        with nc.allow_non_contiguous_dma(reason="one bias value for each partition"):
            nc.sync.dma_start(bias_t[:], bias.rearrange("(c p) -> p c", p=P))

        first_stage(0, 2)
        round_w1_in_pieces((1, 1))
        cap_t[1] = load_rows(streamed([P, PACK, M], F32, "cap1"), cap, 1, 0, M)
        quantize_w1((1, 1), 0, PACK)
        first_stage(0, 3)
        for t in range(PACK):
            subtract_pairs(0, t)

        for t in range(PACK):
            if t == PACK // 2:
                first_stage(1, 0)
            for u in units[:2]:
                take_abs(u, t)
        first_stage(1, 1)
        for u in units[:2]:
            round_low(u)
        for u in units[:2]:
            round_dif(u)
        first_stage(1, 2)
        for b in range(2):
            nc.scalar.copy(pairs_out(w3_bf[:, b, :, :]), pairs_in(w3_raw[:, b, :, :]))
        first_stage(1, 3)
        w3_flat = w3_bf[:].rearrange("p b n j -> p (b n j)")
        for lo, hi in ((0, PASS), (PASS, 2 * N)):
            quantize(w3_codes[:, lo:hi], w3_planes[:, lo:hi], w3_flat[:, PACK * lo : PACK * hi])
        for u in units[:2]:
            quantize_unit(low_codes, low_planes, low_bf, u)
            quantize_unit(dif_codes, dif_planes, dif_bf, u)
        for half in range(2):
            for c in range(N // P):
                second_stage(0, half, c)

        for t in range(PACK):
            subtract_pairs(1, t)
        for t in range(PACK - 1):
            for u in units[2:]:
                take_abs(u, t)
        for u in units[2:]:
            take_abs(u, PACK - 1)
            round_dif(u)
        for u in units[2:]:
            round_low(u)
            quantize_unit(dif_codes, dif_planes, dif_bf, u)
            quantize_unit(low_codes, low_planes, low_bf, u)
        for half in range(2):
            finish(half)
